import numpy as np
import ml_dtypes


def mxq(x, axis, fmt="e4m3"):
    dtype, down = {"e4m3": (ml_dtypes.float8_e4m3fn, 7), "e5m2": (ml_dtypes.float8_e5m2, 14)}[fmt]
    v = np.moveaxis(np.asarray(x, np.float32).astype(ml_dtypes.bfloat16).astype(np.float64), axis, -1)
    blocks = v.reshape(v.shape[:-1] + (-1, 32))
    amax = np.abs(blocks).max(-1, keepdims=True)
    byte = np.maximum(np.where(amax > 0, np.frexp(amax)[1] - 1 + 127, 0) - down, 1)
    scale = np.exp2(byte - 127.0)
    codes = (blocks / scale).astype(np.float32).astype(dtype).astype(np.float64)
    return np.moveaxis((codes * scale).reshape(v.shape), -1, axis)


WIDE = False


def mx_kscale(k):
    if not WIDE:
        return np.ones(k)
    levels = np.array([10, -10, 5, -5, 0])
    if k % 512:
        return np.exp2(np.random.permutation(np.resize(levels, k // 32))).repeat(32)
    a = np.empty((k // 512, 16))
    for p in range(k // 512):
        a[p, :8] = np.random.permutation(np.resize(levels, 8))
        for g in range(8):
            far = levels[np.abs(levels - a[p, g]) >= 10]
            a[p, g + 8] = far[np.random.randint(len(far))]
    return np.exp2(a.ravel()).repeat(32)


def f64(x):
    return np.asarray(x).astype(np.float64)


def striped(idx):
    return np.tile(idx.reshape(-1, 16).T, (8, 1)).astype(np.uint16)


def unstriped(offs):
    return offs[:16].T.reshape(-1).astype(np.int64)


def striped8(idx):
    return np.concatenate([x.reshape(-1, 16).T for x in idx]).astype(np.uint16)


def runs(offs, k):
    lists = np.stack([offs[16 * r : 16 * r + 16].T.reshape(-1) for r in range(8)]).astype(np.int64)
    return lists[np.arange(k) % 512 // 64]


def pack_weight(w):
    k, n = w.shape
    w = f64(np.asarray(w, np.float32).astype(ml_dtypes.bfloat16)).reshape(k // 32, 32, n)
    amax = np.abs(w).max(1)
    byte = np.clip(np.where(amax > 0, np.frexp(amax)[1] - 1 + 127 - 7, 1), 1, 254)
    scaled = (w * np.exp2(127.0 - byte)[:, None, :]).reshape(k, n).astype(np.float32)
    words = np.ascontiguousarray(scaled.reshape(k // 512, 128, 4, n).transpose(0, 1, 3, 2)).astype(ml_dtypes.float8_e4m3fn).view(np.uint8)
    return words, np.ascontiguousarray(byte.astype(np.uint8).reshape(k // 512, 16, n))


def unpack_weight(words, scales):
    g, p, n, _ = words.shape
    vals = np.ascontiguousarray(words).view(ml_dtypes.float8_e4m3fn).astype(np.float64) * np.repeat(np.exp2(scales.astype(np.float64) - 127.0), 8, axis=1)[..., None]
    return vals.transpose(0, 1, 3, 2).reshape(g * 512, n)


E2M1 = np.array([0.0, 0.5, 1.0, 1.5, 2.0, 3.0, 4.0, 6.0, -0.0, -0.5, -1.0, -1.5, -2.0, -3.0, -4.0, -6.0])


def pack_fp4(w):
    k, n = w.shape
    w = f64(np.asarray(w, np.float32).astype(ml_dtypes.bfloat16)).reshape(k // 32, 32, n)
    amax = np.abs(w).max(1)
    mant, ex = np.frexp(amax / 6.0)
    byte = np.clip(np.where(amax > 0, np.where(mant > 0.5, ex, ex - 1) + 127, 1), 1, 254)
    scaled = (w * np.exp2(127.0 - byte)[:, None, :]).reshape(k, n).astype(np.float32)
    c = np.ascontiguousarray(scaled.reshape(k // 512, 128, 4, n).transpose(0, 1, 3, 2)).astype(ml_dtypes.float4_e2m1fn).view(np.uint8) & 0xF
    words = (c[..., 0::2] | (c[..., 1::2] << 4)).reshape(k // 512, 128, 2 * n)
    return np.ascontiguousarray(words), np.ascontiguousarray(byte.astype(np.uint8).reshape(k // 512, 16, n))


def unpack_fp4(words, scales):
    g, _, n = scales.shape
    words = np.ascontiguousarray(words).reshape(g, 128, n, 2)
    nib = np.empty((g, 128, n, 4), np.uint8)
    nib[..., 0::2] = words & 0xF
    nib[..., 1::2] = words >> 4
    vals = E2M1[nib] * np.repeat(np.exp2(scales.astype(np.float64) - 127.0), 8, axis=1)[..., None]
    return vals.transpose(0, 1, 3, 2).reshape(g * 512, n)


def sigmoid(v):
    return 1.0 / (1.0 + np.exp(-np.maximum(v, -700.0)))

def planes(y):
    n, m = y.shape
    v = y.astype(np.float32).astype(ml_dtypes.bfloat16).astype(np.float64).reshape(n // 32, 32, m)
    top = np.abs(v).max(1)
    byte = np.clip(np.where(top > 0, np.frexp(top)[1] - 1 + 127 - 7, 1), 1, 254)
    codes = (v * np.exp2(127.0 - byte)[:, None, :]).reshape(n, m).astype(np.float32).astype(ml_dtypes.float8_e4m3fn).view(np.uint8)
    words = codes.reshape(n // 512, 128, 4, m).transpose(0, 1, 3, 2)
    return np.ascontiguousarray(words), np.ascontiguousarray(byte.astype(np.uint8).reshape(n // 512, 16, m))


K, T, S, N, H, C = 512, 2048, 512, 512, 512, 512


def setup_inputs():
    n = np.random.standard_normal
    s = mx_kscale(K)[:, None]
    u = mx_kscale(S)
    packed_xT = pack_weight(n((K, T)) * s)
    packed_w1 = pack_fp4(n((K, H)) / np.sqrt(K) / s)
    packed_w2 = pack_fp4(n((K, H)) / np.sqrt(K) / s)
    packed_w3 = pack_fp4(n((H, N)) / np.sqrt(H) / u[:, None])
    return {
        "x_words": packed_xT[0],
        "x_scales": packed_xT[1],
        "w1_words": packed_w1[0],
        "w1_scales": packed_w1[1],
        "w2_words": packed_w2[0],
        "w2_scales": packed_w2[1],
        "gn": (np.random.uniform(0.5, 1.5, (H, 1)) * u[:, None]).astype(np.float32),
        "w3_words": packed_w3[0],
        "w3_scales": packed_w3[1],
        "gs": (np.random.uniform(0.5, 1.5, (K, 1)) / s).astype(np.float32),
        "offs": striped(np.random.permutation(T)[:S]),
        "two": striped(np.random.permutation(T)[:S]),
        "n1": striped8(np.stack([np.random.permutation(S) for _ in range(8)])),
        "n2": striped8(np.stack([np.random.permutation(S) for _ in range(8)])),
        "n3": striped8(np.stack([np.random.permutation(S) for _ in range(8)])),
        "n4": striped8(np.stack([np.random.permutation(S) for _ in range(8)])),
        "cand": striped(np.random.permutation(T)[:C]),
        "n5": striped8(np.stack([np.random.permutation(S) for _ in range(8)])),
        "n6": striped8(np.stack([np.random.permutation(S) for _ in range(8)])),
    }


def reference(x_words, x_scales, w1_words, w1_scales, w2_words, w2_scales, gn, w3_words, w3_scales, gs, offs, two, n1, n2, n3, n4, cand, n5, n6):
    xq = unpack_weight(x_words, x_scales)[:, unstriped(offs)]
    y = unpack_fp4(w1_words, w1_scales).T @ xq
    st = y * (sigmoid(y[np.arange(H)[:, None], runs(n1, H)]))
    z = f64(gn) * (st - (st[np.arange(H)[:, None], runs(n2, H)]))
    a = unpack_fp4(w3_words, w3_scales).T @ mxq(z, 0, "e4m3")
    x_cand = unpack_weight(x_words, x_scales)[:, unstriped(cand)]
    x_two = unpack_weight(x_words, x_scales)[:, unstriped(two)]
    d = unpack_fp4(w2_words, w2_scales).T @ x_two
    pa = d[np.arange(H)[:, None], runs(n3, H)]
    kr = np.exp(-0.5 * ((d - pa) ** 2))
    pb = d[np.arange(H)[:, None], runs(n4, H)]
    kr2 = np.exp(-0.5 * ((d - pb) ** 2))
    z2 = f64(gs) * ((kr * pa + kr2 * pb) / (kr + kr2 + 0.5))
    b = 0.0625 * ((x_cand.T @ mxq(z2, 0, "e4m3")))
    out_0 = (a + a[np.arange(N)[:, None], runs(n5, N)]) * (sigmoid(b + b[np.arange(C)[:, None], runs(n6, C)]))
    return (out_0,) + planes(out_0)

@@ -1,0 +1,240 @@
+from contextlib import ExitStack
+
+import concourse.mybir as mybir
+
+K, T, S = 512, 2048, 512
+FLOPS = 4 * 2 * K * S * S
+
+F32 = mybir.dt.float32
+BF16 = mybir.dt.bfloat16
+I32 = mybir.dt.int32
+U32 = mybir.dt.uint32
+U16 = mybir.dt.uint16
+U8 = mybir.dt.uint8
+FP8X4 = mybir.dt.float8_e4m3fn_x4
+FP4X4 = mybir.dt.float4_e2m1fn_x4
+ALU = mybir.AluOpType
+ACT = mybir.ActivationFunctionType
+
+P = 128
+PACK = 4
+HALF = S // 2
+HALVES = range(2)
+TILES = range(PACK)
+
+
+def tile_picked_tfcdtriebhopgkern_none_po_kernel(
+    tc, x_words, x_scales, w1_words, w1_scales, w2_words, w2_scales, gn, w3_words, w3_scales, gs,
+    offs, two, n1, n2, n3, n4, cand, n5, n6, out_0, out_1, out_2,
+):
+    nc = tc.nc
+    with ExitStack() as ctx:
+        held = ctx.enter_context(tc.tile_pool(name="held", bufs=1))
+        work = ctx.enter_context(tc.tile_pool(name="work", bufs=1))
+        psum = ctx.enter_context(tc.psum_pool(name="psum", bufs=1))
+
+        def cols(h):
+            return slice(h * HALF, (h + 1) * HALF)
+
+        def load_list(src, name):
+            tile = held.tile([P, S // 16], U16, name=name)
+            nc.sync.dma_start(tile[:], src)
+            return tile
+
+        def load_scale_rows(tile, src):
+            nc.vector.memset(tile[:].bitcast(I32), 0)
+            for q in range(4):
+                nc.sync.dma_start(tile[32 * q : 32 * q + 4, :].bitcast(I32), src[0, 4 * q : 4 * q + 4, :].bitcast(I32))
+
+        def load_weight(words, scales, name):
+            raw_words = held.tile([P, 2 * S], U8, name=name + "_raw_words")
+            nc.sync.dma_start(raw_words[:].bitcast(I32), words[0].bitcast(I32))
+            raw_scales = held.tile([P, S], U8, name=name + "_raw_scales")
+            load_scale_rows(raw_scales, scales)
+            return raw_words, raw_scales
+
+        def deal_weight(raw, name):
+            raw_words, raw_scales = raw
+            words = held.tile([P, 2 * S], U8, name=name + "_words", align_bytes=64)
+            nc.scalar.copy(
+                words[:].bitcast(U16).rearrange("p (t m) -> p t m", t=PACK),
+                raw_words[:].bitcast(U16).rearrange("p (m t) -> p t m", t=PACK),
+            )
+            scales = held.tile([P, S], U8, name=name + "_scales", align_bytes=64)
+            nc.vector.tensor_copy(
+                scales[:].rearrange("p (t m) -> p t m", t=PACK),
+                raw_scales[:].rearrange("p (m t) -> p t m", t=PACK),
+            )
+            return words, scales
+
+        def load_row_factor(src, name):
+            tile = held.tile([P, PACK], F32, name=name)
+            nc.sync.dma_start(tile[:], src.rearrange("(p t) one -> p (t one)", t=PACK))
+            return tile
+
+        def half_list(lst, h):
+            return lst[:, h * HALF // 16 : (h + 1) * HALF // 16]
+
+        def planes(name, dtype=F32, width=S, tag=None):
+            return [work.tile([P, width], dtype, name="%s%d" % (name, t), tag="%s%d" % (tag or name, t)) for t in TILES]
+
+        def banks(first, name):
+            return [psum.tile([P, S], F32, name="%s%d" % (name, t), tag="bank%d" % (first + t)) for t in TILES]
+
+        def quantise_half(rows, grouped, codes, scales, h):
+            nc.vector.tensor_copy(grouped[:, cols(h), :], rows[:, :, cols(h)].rearrange("p t j -> p j t"))
+            nc.vector.quantize_mx(
+                out=codes[:, cols(h)].bitcast(FP8X4),
+                scales=scales[:, cols(h)],
+                in_=grouped[:, cols(h), :].rearrange("p j t -> p (j t)"),
+            )
+
+        two_l = load_list(two, "two_l")
+        xs = held.tile([P, T], U8, name="xs")
+        load_scale_rows(xs, x_scales)
+        xw = held.tile([P, T], U32, name="xw")
+        nc.sync.dma_start(xw[:].bitcast(I32), x_words[0].rearrange("p n t -> p (n t)").bitcast(I32))
+        w2_raw = load_weight(w2_words, w2_scales, "w2")
+        offs_l = load_list(offs, "offs_l")
+        cand_l = load_list(cand, "cand_l")
+        n3_l = load_list(n3, "n3_l")
+        n4_l = load_list(n4, "n4_l")
+        w1_raw = load_weight(w1_words, w1_scales, "w1")
+        n1_l = load_list(n1, "n1_l")
+        gn_t = load_row_factor(gn, "gn_t")
+        n2_l = load_list(n2, "n2_l")
+        gs_t = load_row_factor(gs, "gs_t")
+        w3_raw = load_weight(w3_words, w3_scales, "w3")
+        n6_l = load_list(n6, "n6_l")
+        n5_l = load_list(n5, "n5_l")
+
+        def pick(table, lst, dtype, name):
+            picked = held.tile([P, S], dtype, name=name, align_bytes=64)
+            nc.vector.tensor_copy(picked[:], table[:].indirect(lst[:]))
+            return picked
+
+        def pick_dealt(table, lst, dtype, name):
+            picked = held.tile([P, S], dtype, name=name, align_bytes=64)
+            nc.vector.tensor_copy(picked[:].rearrange("p (t m) -> p m t", t=PACK), table[:].indirect(lst[:]))
+            return picked
+
+        two_scales = pick(xs, two_l, U8, "two_scales")
+        two_words = pick(xw, two_l, U32, "two_words")
+        w2_w, w2_s = deal_weight(w2_raw, "w2")
+        d_ps = banks(0, "d_ps")
+        for t in TILES:
+            nc.tensor.matmul_mx(
+                out=d_ps[t][:], lhsT=w2_w[:, 2 * P * t : 2 * P * (t + 1)].bitcast(FP4X4), lhsT_scale=w2_s[:, P * t : P * (t + 1)],
+                rhs=two_words[:].bitcast(FP8X4), rhs_scale=two_scales[:], start=True, stop=True,
+            )
+        idx_scales = pick(xs, offs_l, U8, "idx_scales")
+        idx_words = pick(xw, offs_l, U32, "idx_words")
+        w1_w, w1_s = deal_weight(w1_raw, "w1")
+        y_ps = banks(4, "y_ps")
+        for t in TILES:
+            nc.tensor.matmul_mx(
+                out=y_ps[t][:], lhsT=w1_w[:, 2 * P * t : 2 * P * (t + 1)].bitcast(FP4X4), lhsT_scale=w1_s[:, P * t : P * (t + 1)],
+                rhs=idx_words[:].bitcast(FP8X4), rhs_scale=idx_scales[:], start=True, stop=True,
+            )
+        cand_scales = pick_dealt(xs, cand_l, U8, "cand_scales")
+        cand_words = pick_dealt(xw, cand_l, U32, "cand_words")
+        w3_w, w3_s = deal_weight(w3_raw, "w3")
+
+        d = planes("d")
+        near = planes("near", width=2 * S)
+        gap = planes("gap", width=2 * S)
+        kern = planes("kern", width=2 * S)
+        num = work.tile([P, PACK, S], F32, name="num")
+        den = work.tile([P, PACK, S], F32, name="den")
+        for t in TILES:
+            nc.scalar.copy(d[t][:], d_ps[t][:])
+            for h in HALVES:
+                nc.scalar.activation(near[t][:, cols(h)], d[t][:].indirect(half_list(n3_l, h)), ACT.Copy)
+            for h in HALVES:
+                nc.vector.tensor_copy(near[t][:, cols(2 + h)], d[t][:].indirect(half_list(n4_l, h)))
+            for u in range(2):
+                nc.vector.tensor_tensor(gap[t][:, u * S : (u + 1) * S], near[t][:, u * S : (u + 1) * S], d[t][:], ALU.subtract)
+            nc.scalar.activation(gap[t][:], gap[t][:], ACT.Square)
+            nc.scalar.activation(kern[t][:], gap[t][:], ACT.Exp, scale=-0.5)
+            nc.vector.tensor_tensor(den[:, t, :], kern[t][:, :S], kern[t][:, S:], ALU.add)
+            nc.vector.tensor_tensor(near[t][:], near[t][:], kern[t][:], ALU.mult)
+            nc.vector.tensor_tensor(num[:, t, :], near[t][:, :S], near[t][:, S:], ALU.add)
+
+        th = planes("th")
+        for t in TILES:
+            nc.scalar.activation(th[t][:], y_ps[t][:], ACT.Tanh, scale=0.5)
+        half_bias = held.tile([P, 1], F32, name="half_bias")
+        nc.vector.memset(half_bias[:], 0.5)
+        nc.scalar.activation(den[:], den[:], ACT.Ln, bias=half_bias[:])
+        for h in HALVES:
+            nc.scalar.activation(den[:, :, cols(h)], den[:, :, cols(h)], ACT.Exp, scale=-1.0)
+
+        sig = planes("sig")
+        st = planes("st")
+        for t in TILES:
+            for h in HALVES:
+                nc.vector.tensor_scalar(sig[t][:, cols(h)], th[t][:].indirect(half_list(n1_l, h)), 0.5, 0.5, ALU.mult, ALU.add)
+            nc.vector.scalar_tensor_tensor(st[t][:], y_ps[t][:], gn_t[:, t : t + 1], sig[t][:], ALU.mult, ALU.mult)
+
+        z2 = work.tile([P, PACK, S], BF16, name="z2")
+        z2_grouped = work.tile([P, S, PACK], BF16, name="z2_grouped", align_bytes=64)
+        z2_codes = work.tile([P, S], U32, name="z2_codes", align_bytes=64)
+        z2_scales = work.tile([P, S], U8, name="z2_scales", align_bytes=64)
+        b_ps = banks(0, "b_ps")
+        b = planes("b", tag="d")
+        for h in HALVES:
+            for t in TILES:
+                nc.vector.scalar_tensor_tensor(z2[:, t, cols(h)], num[:, t, cols(h)], gs_t[:, t : t + 1], den[:, t, cols(h)], ALU.mult, ALU.mult)
+            quantise_half(z2, z2_grouped, z2_codes, z2_scales, h)
+            for t in TILES:
+                nc.tensor.matmul_mx(
+                    out=b_ps[t][:, cols(h)], lhsT=cand_words[:, P * t : P * (t + 1)].bitcast(FP8X4), lhsT_scale=cand_scales[:, P * t : P * (t + 1)],
+                    rhs=z2_codes[:, cols(h)].bitcast(FP8X4), rhs_scale=z2_scales[:, cols(h)], start=True, stop=True,
+                )
+
+        st_near = planes("st_near", tag="sig")
+        z = work.tile([P, PACK, S], BF16, name="z")
+        z_grouped = work.tile([P, S, PACK], BF16, name="z_grouped", align_bytes=64)
+        z_codes = work.tile([P, S], U32, name="z_codes", align_bytes=64)
+        z_scales = work.tile([P, S], U8, name="z_scales", align_bytes=64)
+        a_ps = banks(4, "a_ps")
+        for h in HALVES:
+            for t in TILES:
+                nc.scalar.activation(st_near[t][:, cols(h)], st[t][:].indirect(half_list(n2_l, h)), ACT.Copy)
+                nc.vector.tensor_tensor(z[:, t, cols(h)], st[t][:, cols(h)], st_near[t][:, cols(h)], ALU.subtract)
+            quantise_half(z, z_grouped, z_codes, z_scales, h)
+            for t in TILES:
+                nc.tensor.matmul_mx(
+                    out=a_ps[t][:, cols(h)], lhsT=w3_w[:, 2 * P * t : 2 * P * (t + 1)].bitcast(FP4X4), lhsT_scale=w3_s[:, P * t : P * (t + 1)],
+                    rhs=z_codes[:, cols(h)].bitcast(FP8X4), rhs_scale=z_scales[:, cols(h)], start=True, stop=True,
+                )
+
+        b_near = planes("b_near")
+        gate = planes("gate")
+        for t in TILES:
+            nc.scalar.copy(b[t][:], b_ps[t][:])
+            for h in HALVES:
+                nc.scalar.activation(b_near[t][:, cols(h)], b[t][:].indirect(half_list(n6_l, h)), ACT.Copy)
+            nc.vector.tensor_tensor(b_near[t][:], b_near[t][:], b[t][:], ALU.add)
+            nc.scalar.activation(gate[t][:], b_near[t][:], ACT.Tanh, scale=0.0625 * 0.5)
+
+        a = planes("a", tag="th")
+        a_near = planes("a_near")
+        res = work.tile([P, PACK, S], F32, name="res")
+        res_grouped = work.tile([P, S, PACK], BF16, name="res_grouped", align_bytes=64)
+        res_codes = work.tile([P, S], U32, name="res_codes", align_bytes=64)
+        res_scales = work.tile([P, S], U8, name="res_scales", align_bytes=64)
+        out_rows = out_0.rearrange("(p t) j -> p t j", t=PACK)
+        out_words = out_1[0].rearrange("p n t -> p (n t)").bitcast(I32)
+        for t in TILES:
+            nc.scalar.activation(a[t][:], a_ps[t][:], ACT.Copy, scale=0.5)
+        for h in HALVES:
+            for t in TILES:
+                nc.scalar.activation(a_near[t][:, cols(h)], a[t][:].indirect(half_list(n5_l, h)), ACT.Copy)
+                nc.vector.tensor_tensor(a_near[t][:, cols(h)], a_near[t][:, cols(h)], a[t][:, cols(h)], ALU.add)
+                nc.vector.scalar_tensor_tensor(res[:, t, cols(h)], gate[t][:, cols(h)], 1.0, a_near[t][:, cols(h)], ALU.add, ALU.mult)
+            nc.sync.dma_start(out_rows[:, :, cols(h)], res[:, :, cols(h)])
+            quantise_half(res, res_grouped, res_codes, res_scales, h)
+            nc.sync.dma_start(out_words[:, cols(h)], res_codes[:, cols(h)].bitcast(I32))
+        for q in range(4):
+            nc.scalar.dma_start(out_2[0, 4 * q : 4 * q + 4, :].bitcast(I32), res_scales[32 * q : 32 * q + 4, :].bitcast(I32))

@@ -1,6 +1,7 @@
 from contextlib import ExitStack
 
 import concourse.mybir as mybir
+from concourse.masks import make_identity
 
 K, T, S = 512, 2048, 512
 FLOPS = 4 * 2 * K * S * S
@@ -21,6 +22,8 @@ PACK = 4
 HALF = S // 2
 HALVES = range(2)
 TILES = range(PACK)
+BLOCKS = range(S // P)
+ON_SCALAR = {"n3": 8, "n4": 0, "n2": 6, "n6": 2, "n5": 4}
 
 
 def tile_picked_tfcdtriebhopgkern_none_po_kernel(
@@ -46,26 +49,27 @@ def tile_picked_tfcdtriebhopgkern_none_po_kernel(
             for q in range(4):
                 nc.sync.dma_start(tile[32 * q : 32 * q + 4, :].bitcast(I32), src[0, 4 * q : 4 * q + 4, :].bitcast(I32))
 
-        def load_weight(words, scales, name):
-            raw_words = held.tile([P, 2 * S], U8, name=name + "_raw_words")
-            nc.sync.dma_start(raw_words[:].bitcast(I32), words[0].bitcast(I32))
-            raw_scales = held.tile([P, S], U8, name=name + "_raw_scales")
-            load_scale_rows(raw_scales, scales)
-            return raw_words, raw_scales
+        def load_words(words, name):
+            raw = held.tile([P, 2 * S], U8, name=name)
+            nc.sync.dma_start(raw[:].bitcast(I32), words[0].bitcast(I32))
+            return raw
 
-        def deal_weight(raw, name):
-            raw_words, raw_scales = raw
-            words = held.tile([P, 2 * S], U8, name=name + "_words", align_bytes=64)
+        def load_scales(scales, name):
+            raw = held.tile([P, S], U8, name=name)
+            load_scale_rows(raw, scales)
+            return raw
+
+        def deal_words(raw, name):
+            words = held.tile([P, 2 * S], U8, name=name, align_bytes=64)
             nc.scalar.copy(
-                words[:].bitcast(U16).rearrange("p (t m) -> p t m", t=PACK),
-                raw_words[:].bitcast(U16).rearrange("p (m t) -> p t m", t=PACK),
+                words[:].bitcast(U16).rearrange("p (t m) -> p t m", t=PACK), raw[:].bitcast(U16).rearrange("p (m t) -> p t m", t=PACK),
             )
-            scales = held.tile([P, S], U8, name=name + "_scales", align_bytes=64)
-            nc.vector.tensor_copy(
-                scales[:].rearrange("p (t m) -> p t m", t=PACK),
-                raw_scales[:].rearrange("p (m t) -> p t m", t=PACK),
-            )
-            return words, scales
+            return words
+
+        def deal_scales(raw, name):
+            scales = held.tile([P, S], U8, name=name, align_bytes=64)
+            nc.vector.tensor_copy(scales[:].rearrange("p (t m) -> p t m", t=PACK), raw[:].rearrange("p (m t) -> p t m", t=PACK))
+            return scales
 
         def load_row_factor(src, name):
             tile = held.tile([P, PACK], F32, name=name)
@@ -81,32 +85,55 @@ def tile_picked_tfcdtriebhopgkern_none_po_kernel(
         def banks(first, name):
             return [psum.tile([P, S], F32, name="%s%d" % (name, t), tag="bank%d" % (first + t)) for t in TILES]
 
-        def quantise_half(rows, grouped, codes, scales, h):
-            nc.vector.tensor_copy(grouped[:, cols(h), :], rows[:, :, cols(h)].rearrange("p t j -> p j t"))
+        def quantise_half(rows, grouped, codes, scales, h, move=nc.vector.tensor_copy):
+            move(grouped[:, cols(h), :], rows[:, :, cols(h)].rearrange("p t j -> p j t"))
             nc.vector.quantize_mx(
                 out=codes[:, cols(h)].bitcast(FP8X4),
                 scales=scales[:, cols(h)],
                 in_=grouped[:, cols(h), :].rearrange("p j t -> p (j t)"),
             )
 
+        def fetch(name, out, window, lst, h, turn):
+            piece = window[:].indirect(half_list(lst, h))
+            if (turn + 1) * ON_SCALAR[name] // 8 > turn * ON_SCALAR[name] // 8:
+                nc.scalar.activation(out, piece, ACT.Copy)
+            else:
+                nc.vector.tensor_copy(out, piece)
+
+        def blk(jb):
+            return slice(jb * P, (jb + 1) * P)
+
+        def turn_sum(out, first, second):
+            nc.tensor.matmul(out, first, ident[:], start=True, stop=False, is_transpose=True)
+            nc.tensor.matmul(out, second, ident[:], start=False, stop=True, is_transpose=True)
+
+        ident = held.tile([P, P], F32, name="ident")
+        make_identity(nc, ident[:])
+
         two_l = load_list(two, "two_l")
+        offs_l = load_list(offs, "offs_l")
         xs = held.tile([P, T], U8, name="xs")
         load_scale_rows(xs, x_scales)
         xw = held.tile([P, T], U32, name="xw")
         nc.sync.dma_start(xw[:].bitcast(I32), x_words[0].rearrange("p n t -> p (n t)").bitcast(I32))
-        w2_raw = load_weight(w2_words, w2_scales, "w2")
-        offs_l = load_list(offs, "offs_l")
-        cand_l = load_list(cand, "cand_l")
+        w2_raw = load_words(w2_words, "w2_raw")
+        w2_raw_s = load_scales(w2_scales, "w2_raw_s")
+        w1_raw = load_words(w1_words, "w1_raw")
+        w3_raw = load_words(w3_words, "w3_raw")
         n3_l = load_list(n3, "n3_l")
         n4_l = load_list(n4, "n4_l")
-        w1_raw = load_weight(w1_words, w1_scales, "w1")
+        w1_raw_s = load_scales(w1_scales, "w1_raw_s")
+        cand_l = load_list(cand, "cand_l")
+        gs_t = load_row_factor(gs, "gs_t")
         n1_l = load_list(n1, "n1_l")
         gn_t = load_row_factor(gn, "gn_t")
         n2_l = load_list(n2, "n2_l")
-        gs_t = load_row_factor(gs, "gs_t")
-        w3_raw = load_weight(w3_words, w3_scales, "w3")
+        w3_raw_s = load_scales(w3_scales, "w3_raw_s")
         n6_l = load_list(n6, "n6_l")
         n5_l = load_list(n5, "n5_l")
+        w2_w = deal_words(w2_raw, "w2_w")
+        w1_w = deal_words(w1_raw, "w1_w")
+        w3_w = deal_words(w3_raw, "w3_w")
 
         def pick(table, lst, dtype, name):
             picked = held.tile([P, S], dtype, name=name, align_bytes=64)
@@ -118,123 +145,183 @@ def tile_picked_tfcdtriebhopgkern_none_po_kernel(
             nc.vector.tensor_copy(picked[:].rearrange("p (t m) -> p m t", t=PACK), table[:].indirect(lst[:]))
             return picked
 
+        def product(out, words, scales, t, codes, code_scales, fp4=True):
+            width = 2 * P if fp4 else P
+            nc.tensor.matmul_mx(
+                out=out, lhsT=words[:, width * t : width * (t + 1)].bitcast(FP4X4 if fp4 else FP8X4), lhsT_scale=scales[:, blk(t)],
+                rhs=codes.bitcast(FP8X4), rhs_scale=code_scales, start=True, stop=True,
+            )
+
         two_scales = pick(xs, two_l, U8, "two_scales")
         two_words = pick(xw, two_l, U32, "two_words")
-        w2_w, w2_s = deal_weight(w2_raw, "w2")
+        w2_s = deal_scales(w2_raw_s, "w2_s")
         d_ps = banks(0, "d_ps")
         for t in TILES:
-            nc.tensor.matmul_mx(
-                out=d_ps[t][:], lhsT=w2_w[:, 2 * P * t : 2 * P * (t + 1)].bitcast(FP4X4), lhsT_scale=w2_s[:, P * t : P * (t + 1)],
-                rhs=two_words[:].bitcast(FP8X4), rhs_scale=two_scales[:], start=True, stop=True,
-            )
+            product(d_ps[t][:], w2_w, w2_s, t, two_words[:], two_scales[:])
         idx_scales = pick(xs, offs_l, U8, "idx_scales")
         idx_words = pick(xw, offs_l, U32, "idx_words")
-        w1_w, w1_s = deal_weight(w1_raw, "w1")
+        w1_s = deal_scales(w1_raw_s, "w1_s")
         y_ps = banks(4, "y_ps")
         for t in TILES:
-            nc.tensor.matmul_mx(
-                out=y_ps[t][:], lhsT=w1_w[:, 2 * P * t : 2 * P * (t + 1)].bitcast(FP4X4), lhsT_scale=w1_s[:, P * t : P * (t + 1)],
-                rhs=idx_words[:].bitcast(FP8X4), rhs_scale=idx_scales[:], start=True, stop=True,
-            )
-        cand_scales = pick_dealt(xs, cand_l, U8, "cand_scales")
-        cand_words = pick_dealt(xw, cand_l, U32, "cand_words")
-        w3_w, w3_s = deal_weight(w3_raw, "w3")
+            product(y_ps[t][:], w1_w, w1_s, t, idx_words[:], idx_scales[:])
 
         d = planes("d")
         near = planes("near", width=2 * S)
         gap = planes("gap", width=2 * S)
         kern = planes("kern", width=2 * S)
-        num = work.tile([P, PACK, S], F32, name="num")
-        den = work.tile([P, PACK, S], F32, name="den")
-        for t in TILES:
-            nc.scalar.copy(d[t][:], d_ps[t][:])
-            for h in HALVES:
-                nc.scalar.activation(near[t][:, cols(h)], d[t][:].indirect(half_list(n3_l, h)), ACT.Copy)
-            for h in HALVES:
-                nc.vector.tensor_copy(near[t][:, cols(2 + h)], d[t][:].indirect(half_list(n4_l, h)))
-            for u in range(2):
-                nc.vector.tensor_tensor(gap[t][:, u * S : (u + 1) * S], near[t][:, u * S : (u + 1) * S], d[t][:], ALU.subtract)
-            nc.scalar.activation(gap[t][:], gap[t][:], ACT.Square)
-            nc.scalar.activation(kern[t][:], gap[t][:], ACT.Exp, scale=-0.5)
-            nc.vector.tensor_tensor(den[:, t, :], kern[t][:, :S], kern[t][:, S:], ALU.add)
-            nc.vector.tensor_tensor(near[t][:], near[t][:], kern[t][:], ALU.mult)
-            nc.vector.tensor_tensor(num[:, t, :], near[t][:, :S], near[t][:, S:], ALU.add)
-
         th = planes("th")
-        for t in TILES:
-            nc.scalar.activation(th[t][:], y_ps[t][:], ACT.Tanh, scale=0.5)
-        half_bias = held.tile([P, 1], F32, name="half_bias")
-        nc.vector.memset(half_bias[:], 0.5)
-        nc.scalar.activation(den[:], den[:], ACT.Ln, bias=half_bias[:])
-        for h in HALVES:
-            nc.scalar.activation(den[:, :, cols(h)], den[:, :, cols(h)], ACT.Exp, scale=-1.0)
-
         sig = planes("sig")
         st = planes("st")
-        for t in TILES:
+        st_near = planes("st_near")
+        inv = planes("inv")
+        z2_turned = planes("z2_turned", dtype=BF16)
+        b = planes("b")
+        b_near = planes("b_near")
+        gate_turned = planes("gate_turned")
+        a = planes("a")
+        a_near = planes("a_near")
+        res = work.tile([P, PACK, S], F32, name="res")
+        z = work.tile([P, PACK, S], BF16, name="z")
+
+        def quantised(name):
+            grouped = work.tile([P, S, PACK], BF16, name=name + "_grouped", align_bytes=64)
+            codes = work.tile([P, S], U32, name=name + "_codes", align_bytes=64)
+            scales = work.tile([P, S], U8, name=name + "_scales", align_bytes=64)
+            return grouped, codes, scales
+
+        z_grouped, z_codes, z_scales = quantised("z")
+        z2_grouped, z2_codes, z2_scales = quantised("z2")
+        res_grouped, res_codes, res_scales = quantised("res")
+        half_bias = held.tile([P, 1], F32, name="half_bias")
+        nc.vector.memset(half_bias[:], 0.5)
+        out_rows = out_0.rearrange("(p t) j -> p t j", t=PACK)
+        out_words = out_1[0].rearrange("p n t -> p (n t)").bitcast(I32)
+
+        def words_order(ap, pattern):
+            return ap.rearrange(pattern + " -> j u p e", u=2, e=2)
+
+        def neighbours(t):
+            for h in HALVES:
+                fetch("n3", near[t][:, cols(h)], d[t], n3_l, h, 2 * t + h)
+            for h in HALVES:
+                fetch("n4", near[t][:, cols(2 + h)], d[t], n4_l, h, 2 * t + h)
+            nc.vector.tensor_tensor(
+                gap[t][:].rearrange("p (u j) -> p u j", u=2), near[t][:].rearrange("p (u j) -> p u j", u=2),
+                d[t][:].unsqueeze(1).to_broadcast([P, 2, S]), ALU.subtract,
+            )
+
+        def kernel_weights(t, den_ps):
+            nc.scalar.activation(gap[t][:], gap[t][:], ACT.Square)
+            nc.scalar.activation(kern[t][:], gap[t][:], ACT.Exp, scale=-0.5)
+            for jb in BLOCKS:
+                turn_sum(den_ps[jb][:, blk(t)], kern[t][:, blk(jb)], kern[t][:, blk(PACK + jb)])
+            nc.vector.scalar_tensor_tensor(near[t][:], near[t][:], gs_t[:, t : t + 1], kern[t][:], ALU.mult, ALU.mult)
+
+        def gated(t):
             for h in HALVES:
                 nc.vector.tensor_scalar(sig[t][:, cols(h)], th[t][:].indirect(half_list(n1_l, h)), 0.5, 0.5, ALU.mult, ALU.add)
             nc.vector.scalar_tensor_tensor(st[t][:], y_ps[t][:], gn_t[:, t : t + 1], sig[t][:], ALU.mult, ALU.mult)
 
-        z2 = work.tile([P, PACK, S], BF16, name="z2")
-        z2_grouped = work.tile([P, S, PACK], BF16, name="z2_grouped", align_bytes=64)
-        z2_codes = work.tile([P, S], U32, name="z2_codes", align_bytes=64)
-        z2_scales = work.tile([P, S], U8, name="z2_scales", align_bytes=64)
-        b_ps = banks(0, "b_ps")
-        b = planes("b", tag="d")
-        for h in HALVES:
-            for t in TILES:
-                nc.vector.scalar_tensor_tensor(z2[:, t, cols(h)], num[:, t, cols(h)], gs_t[:, t : t + 1], den[:, t, cols(h)], ALU.mult, ALU.mult)
-            quantise_half(z2, z2_grouped, z2_codes, z2_scales, h)
-            for t in TILES:
-                nc.tensor.matmul_mx(
-                    out=b_ps[t][:, cols(h)], lhsT=cand_words[:, P * t : P * (t + 1)].bitcast(FP8X4), lhsT_scale=cand_scales[:, P * t : P * (t + 1)],
-                    rhs=z2_codes[:, cols(h)].bitcast(FP8X4), rhs_scale=z2_scales[:, cols(h)], start=True, stop=True,
-                )
+        def inverse(den_ps):
+            for jb in BLOCKS:
+                nc.scalar.activation(words_order(inv[jb][:], "j (u p e)"), words_order(den_ps[jb][:], "j (u e p)"), ACT.Ln, bias=half_bias[:])
+            for jb in BLOCKS:
+                nc.scalar.activation(inv[jb][:], inv[jb][:], ACT.Exp, scale=-1.0)
 
-        st_near = planes("st_near", tag="sig")
-        z = work.tile([P, PACK, S], BF16, name="z")
-        z_grouped = work.tile([P, S, PACK], BF16, name="z_grouped", align_bytes=64)
-        z_codes = work.tile([P, S], U32, name="z_codes", align_bytes=64)
-        z_scales = work.tile([P, S], U8, name="z_scales", align_bytes=64)
-        a_ps = banks(4, "a_ps")
-        for h in HALVES:
-            for t in TILES:
-                nc.scalar.activation(st_near[t][:, cols(h)], st[t][:].indirect(half_list(n2_l, h)), ACT.Copy)
-                nc.vector.tensor_tensor(z[:, t, cols(h)], st[t][:, cols(h)], st_near[t][:, cols(h)], ALU.subtract)
-            quantise_half(z, z_grouped, z_codes, z_scales, h)
-            for t in TILES:
-                nc.tensor.matmul_mx(
-                    out=a_ps[t][:, cols(h)], lhsT=w3_w[:, 2 * P * t : 2 * P * (t + 1)].bitcast(FP4X4), lhsT_scale=w3_s[:, P * t : P * (t + 1)],
-                    rhs=z_codes[:, cols(h)].bitcast(FP8X4), rhs_scale=z_scales[:, cols(h)], start=True, stop=True,
-                )
-
-        b_near = planes("b_near")
-        gate = planes("gate")
-        for t in TILES:
-            nc.scalar.copy(b[t][:], b_ps[t][:])
+        def scores(first_bank):
+            num_ps = banks(0, "num_ps")
+            for jb in BLOCKS:
+                for t in TILES:
+                    turn_sum(num_ps[jb][:, blk(t)], near[t][:, blk(jb)], near[t][:, blk(PACK + jb)])
+            b_ps = banks(4, "b_ps")
             for h in HALVES:
-                nc.scalar.activation(b_near[t][:, cols(h)], b[t][:].indirect(half_list(n6_l, h)), ACT.Copy)
-            nc.vector.tensor_tensor(b_near[t][:], b_near[t][:], b[t][:], ALU.add)
-            nc.scalar.activation(gate[t][:], b_near[t][:], ACT.Tanh, scale=0.0625 * 0.5)
-
-        a = planes("a", tag="th")
-        a_near = planes("a_near")
-        res = work.tile([P, PACK, S], F32, name="res")
-        res_grouped = work.tile([P, S, PACK], BF16, name="res_grouped", align_bytes=64)
-        res_codes = work.tile([P, S], U32, name="res_codes", align_bytes=64)
-        res_scales = work.tile([P, S], U8, name="res_scales", align_bytes=64)
-        out_rows = out_0.rearrange("(p t) j -> p t j", t=PACK)
-        out_words = out_1[0].rearrange("p n t -> p (n t)").bitcast(I32)
-        for t in TILES:
-            nc.scalar.activation(a[t][:], a_ps[t][:], ACT.Copy, scale=0.5)
-        for h in HALVES:
+                for jb in (2 * h, 2 * h + 1):
+                    nc.vector.tensor_tensor(
+                        words_order(z2_turned[jb][:], "j (u p e)"), words_order(num_ps[jb][:], "j (u e p)"),
+                        words_order(inv[jb][:], "j (u p e)"), ALU.mult,
+                    )
+                pairs_ps = psum.tile([P, 2, 2, P], F32, name="pairs_ps%d" % h, tag="bank%d" % (2 * h))
+                for c in range(2):
+                    for u in range(2):
+                        nc.tensor.transpose(pairs_ps[:, c, u, :], z2_turned[2 * h + c][:].bitcast(F32)[:, blk(u)], ident[:])
+                nc.scalar.copy(
+                    z2_grouped[:, cols(h), :].bitcast(F32).rearrange("p (c j) u -> p c j u", c=2), pairs_ps[:].rearrange("p c u j -> p c j u"),
+                )
+                nc.vector.quantize_mx(
+                    out=z2_codes[:, cols(h)].bitcast(FP8X4), scales=z2_scales[:, cols(h)],
+                    in_=z2_grouped[:, cols(h), :].rearrange("p j t -> p (j t)"),
+                )
+                for t in TILES:
+                    product(b_ps[t][:, cols(h)], cand_words, cand_scales, t, z2_codes[:, cols(h)], z2_scales[:, cols(h)], fp4=False)
             for t in TILES:
-                nc.scalar.activation(a_near[t][:, cols(h)], a[t][:].indirect(half_list(n5_l, h)), ACT.Copy)
+                nc.scalar.copy(b[t][:], b_ps[t][:])
+
+        def differences():
+            for h in HALVES:
+                for t in TILES:
+                    fetch("n2", st_near[t][:, cols(h)], st[t], n2_l, h, PACK * h + t)
+                    nc.vector.tensor_tensor(z[:, t, cols(h)], st[t][:, cols(h)], st_near[t][:, cols(h)], ALU.subtract)
+                quantise_half(z, z_grouped, z_codes, z_scales, h)
+
+        def layer():
+            a_ps = banks(4, "a_ps")
+            for h in HALVES:
+                for t in TILES:
+                    product(a_ps[t][:, cols(h)], w3_w, w3_s, t, z_codes[:, cols(h)], z_scales[:, cols(h)])
+            for t in TILES:
+                nc.scalar.activation(a[t][:], a_ps[t][:], ACT.Copy, scale=0.5)
+
+        def gates():
+            b_sum_ps = banks(0, "b_sum_ps")
+            for t in TILES:
+                for h in HALVES:
+                    fetch("n6", b_near[t][:, cols(h)], b[t], n6_l, h, 2 * t + h)
+                for jb in BLOCKS:
+                    turn_sum(b_sum_ps[t][:, blk(jb)], b[t][:, blk(jb)], b_near[t][:, blk(jb)])
+                nc.scalar.activation(gate_turned[t][:], b_sum_ps[t][:], ACT.Tanh, scale=0.0625 * 0.5)
+            gate = banks(0, "gate")
+            for t in TILES:
+                for jb in BLOCKS:
+                    nc.tensor.transpose(gate[t][:, blk(jb)], gate_turned[t][:, blk(jb)], ident[:])
+            return gate
+
+        def pair_sums(h):
+            for t in TILES:
+                fetch("n5", a_near[t][:, cols(h)], a[t], n5_l, h, PACK * h + t)
                 nc.vector.tensor_tensor(a_near[t][:, cols(h)], a_near[t][:, cols(h)], a[t][:, cols(h)], ALU.add)
+
+        def result(h, gate):
+            for t in TILES:
                 nc.vector.scalar_tensor_tensor(res[:, t, cols(h)], gate[t][:, cols(h)], 1.0, a_near[t][:, cols(h)], ALU.add, ALU.mult)
             nc.sync.dma_start(out_rows[:, :, cols(h)], res[:, :, cols(h)])
-            quantise_half(res, res_grouped, res_codes, res_scales, h)
+            quantise_half(res, res_grouped, res_codes, res_scales, h, nc.vector.tensor_copy if h else nc.scalar.copy)
             nc.sync.dma_start(out_words[:, cols(h)], res_codes[:, cols(h)].bitcast(I32))
-        for q in range(4):
-            nc.scalar.dma_start(out_2[0, 4 * q : 4 * q + 4, :].bitcast(I32), res_scales[32 * q : 32 * q + 4, :].bitcast(I32))
+
+        def store_scales():
+            for q in range(4):
+                nc.scalar.dma_start(out_2[0, 4 * q : 4 * q + 4, :].bitcast(I32), res_scales[32 * q : 32 * q + 4, :].bitcast(I32))
+
+        for t in TILES:
+            nc.scalar.copy(d[t][:], d_ps[t][:])
+        den_ps = banks(0, "den_ps")
+        neighbours(0)
+        for t in TILES:
+            if t + 1 < PACK:
+                neighbours(t + 1)
+            kernel_weights(t, den_ps)
+        for t in TILES:
+            nc.scalar.activation(th[t][:], y_ps[t][:], ACT.Tanh, scale=0.5)
+        cand_scales = pick_dealt(xs, cand_l, U8, "cand_scales")
+        cand_words = pick_dealt(xw, cand_l, U32, "cand_words")
+        w3_s = deal_scales(w3_raw_s, "w3_s")
+        inverse(den_ps)
+        for t in TILES:
+            gated(t)
+        scores(0)
+        differences()
+        layer()
+        gate = gates()
+        for h in HALVES:
+            pair_sums(h)
+            result(h, gate)
+        store_scales()

@@ -23,7 +23,7 @@ HALF = S // 2
 HALVES = range(2)
 TILES = range(PACK)
 BLOCKS = range(S // P)
-ON_SCALAR = {"n3": 8, "n4": 0, "n2": 6, "n6": 2, "n5": 4}
+ON_SCALAR = {"n3": 6, "n4": 0, "n2": 2, "n6": 4, "n5": 2, "n1": 0}
 
 
 def tile_picked_tfcdtriebhopgkern_none_po_kernel(
@@ -55,7 +55,7 @@ def tile_picked_tfcdtriebhopgkern_none_po_kernel(
             return raw
 
         def load_scales(scales, name):
-            raw = held.tile([P, S], U8, name=name)
+            raw = held.tile([P, S], U8, name=name, align_bytes=64)
             load_scale_rows(raw, scales)
             return raw
 
@@ -66,9 +66,9 @@ def tile_picked_tfcdtriebhopgkern_none_po_kernel(
             )
             return words
 
-        def deal_scales(raw, name):
+        def deal_scales(raw, name, engine=nc.vector):
             scales = held.tile([P, S], U8, name=name, align_bytes=64)
-            nc.vector.tensor_copy(scales[:].rearrange("p (t m) -> p t m", t=PACK), raw[:].rearrange("p (m t) -> p t m", t=PACK))
+            engine.tensor_copy(scales[:].rearrange("p (t m) -> p t m", t=PACK), raw[:].rearrange("p (m t) -> p t m", t=PACK))
             return scales
 
         def load_row_factor(src, name):
@@ -80,25 +80,30 @@ def tile_picked_tfcdtriebhopgkern_none_po_kernel(
             return lst[:, h * HALF // 16 : (h + 1) * HALF // 16]
 
         def planes(name, dtype=F32, width=S, tag=None):
-            return [work.tile([P, width], dtype, name="%s%d" % (name, t), tag="%s%d" % (tag or name, t)) for t in TILES]
+            return [work.tile([P, width], dtype, name="%s%d" % (name, t), tag="%s%d" % (tag or name, t), align_bytes=64) for t in TILES]
 
         def banks(first, name):
             return [psum.tile([P, S], F32, name="%s%d" % (name, t), tag="bank%d" % (first + t)) for t in TILES]
 
         def quantise_half(rows, grouped, codes, scales, h, move=nc.vector.tensor_copy):
-            move(grouped[:, cols(h), :], rows[:, :, cols(h)].rearrange("p t j -> p j t"))
+            move(grouped[:, cols(h), :], rows[:].rearrange("p t j -> p j t"))
             nc.vector.quantize_mx(
                 out=codes[:, cols(h)].bitcast(FP8X4),
                 scales=scales[:, cols(h)],
                 in_=grouped[:, cols(h), :].rearrange("p j t -> p (j t)"),
             )
 
-        def fetch(name, out, window, lst, h, turn):
+        def fetch(name, out, window, lst, h, turn, scale=None, bias=None):
             piece = window[:].indirect(half_list(lst, h))
-            if (turn + 1) * ON_SCALAR[name] // 8 > turn * ON_SCALAR[name] // 8:
+            on_scalar = (turn + 1) * ON_SCALAR[name] // 8 > turn * ON_SCALAR[name] // 8
+            if scale is None and on_scalar:
                 nc.scalar.activation(out, piece, ACT.Copy)
-            else:
+            elif scale is None:
                 nc.vector.tensor_copy(out, piece)
+            elif on_scalar:
+                nc.scalar.activation(out, piece, ACT.Copy, scale=scale, bias=bias)
+            else:
+                nc.vector.tensor_scalar(out, piece, scale, bias, ALU.mult, ALU.add)
 
         def blk(jb):
             return slice(jb * P, (jb + 1) * P)
@@ -135,13 +140,13 @@ def tile_picked_tfcdtriebhopgkern_none_po_kernel(
         w1_w = deal_words(w1_raw, "w1_w")
         w3_w = deal_words(w3_raw, "w3_w")
 
-        def pick(table, lst, dtype, name):
-            picked = held.tile([P, S], dtype, name=name, align_bytes=64)
+        def pick(table, lst, dtype, name, tag=None):
+            picked = held.tile([P, S], dtype, name=name, tag=tag or name, align_bytes=64)
             nc.vector.tensor_copy(picked[:], table[:].indirect(lst[:]))
             return picked
 
-        def pick_dealt(table, lst, dtype, name):
-            picked = held.tile([P, S], dtype, name=name, align_bytes=64)
+        def pick_dealt(table, lst, dtype, name, tag):
+            picked = work.tile([P, S], dtype, name=name, tag=tag, align_bytes=64)
             nc.vector.tensor_copy(picked[:].rearrange("p (t m) -> p m t", t=PACK), table[:].indirect(lst[:]))
             return picked
 
@@ -159,7 +164,7 @@ def tile_picked_tfcdtriebhopgkern_none_po_kernel(
         for t in TILES:
             product(d_ps[t][:], w2_w, w2_s, t, two_words[:], two_scales[:])
         idx_scales = pick(xs, offs_l, U8, "idx_scales")
-        idx_words = pick(xw, offs_l, U32, "idx_words")
+        idx_words = pick(xw, offs_l, U32, "idx_words", tag="w2_raw_s")
         w1_s = deal_scales(w1_raw_s, "w1_s")
         y_ps = banks(4, "y_ps")
         for t in TILES:
@@ -179,9 +184,8 @@ def tile_picked_tfcdtriebhopgkern_none_po_kernel(
         b_near = planes("b_near")
         gate_turned = planes("gate_turned")
         a = planes("a")
-        a_near = planes("a_near")
+        a_near = work.tile([P, PACK, S], F32, name="a_near")
         res = work.tile([P, PACK, S], F32, name="res")
-        z = work.tile([P, PACK, S], BF16, name="z")
 
         def quantised(name):
             grouped = work.tile([P, S, PACK], BF16, name=name + "_grouped", align_bytes=64)
@@ -207,19 +211,20 @@ def tile_picked_tfcdtriebhopgkern_none_po_kernel(
                 fetch("n4", near[t][:, cols(2 + h)], d[t], n4_l, h, 2 * t + h)
             nc.vector.tensor_tensor(
                 gap[t][:].rearrange("p (u j) -> p u j", u=2), near[t][:].rearrange("p (u j) -> p u j", u=2),
-                d[t][:].unsqueeze(1).to_broadcast([P, 2, S]), ALU.subtract,
+                d_ps[t][:].unsqueeze(1).to_broadcast([P, 2, S]), ALU.subtract,
             )
+            nc.gpsimd.tensor_scalar(near[t][:], near[t][:], gs_t[:, t : t + 1], 0.0, ALU.mult, ALU.add)
 
         def kernel_weights(t, den_ps):
             nc.scalar.activation(gap[t][:], gap[t][:], ACT.Square)
             nc.scalar.activation(kern[t][:], gap[t][:], ACT.Exp, scale=-0.5)
             for jb in BLOCKS:
                 turn_sum(den_ps[jb][:, blk(t)], kern[t][:, blk(jb)], kern[t][:, blk(PACK + jb)])
-            nc.vector.scalar_tensor_tensor(near[t][:], near[t][:], gs_t[:, t : t + 1], kern[t][:], ALU.mult, ALU.mult)
+            nc.gpsimd.tensor_tensor(near[t][:], near[t][:], kern[t][:], ALU.mult)
 
         def gated(t):
             for h in HALVES:
-                nc.vector.tensor_scalar(sig[t][:, cols(h)], th[t][:].indirect(half_list(n1_l, h)), 0.5, 0.5, ALU.mult, ALU.add)
+                fetch("n1", sig[t][:, cols(h)], th[t], n1_l, h, 2 * t + h, 0.5, 0.5)
             nc.vector.scalar_tensor_tensor(st[t][:], y_ps[t][:], gn_t[:, t : t + 1], sig[t][:], ALU.mult, ALU.mult)
 
         def inverse(den_ps):
@@ -233,7 +238,6 @@ def tile_picked_tfcdtriebhopgkern_none_po_kernel(
             for jb in BLOCKS:
                 for t in TILES:
                     turn_sum(num_ps[jb][:, blk(t)], near[t][:, blk(jb)], near[t][:, blk(PACK + jb)])
-            b_ps = banks(4, "b_ps")
             for h in HALVES:
                 for jb in (2 * h, 2 * h + 1):
                     nc.vector.tensor_tensor(
@@ -251,16 +255,18 @@ def tile_picked_tfcdtriebhopgkern_none_po_kernel(
                     out=z2_codes[:, cols(h)].bitcast(FP8X4), scales=z2_scales[:, cols(h)],
                     in_=z2_grouped[:, cols(h), :].rearrange("p j t -> p (j t)"),
                 )
+                b_ps = [psum.tile([P, 2, HALF], F32, name="b_ps%d%d" % (h, c), tag="bank%d" % (2 * h + c)) for c in range(2)]
                 for t in TILES:
-                    product(b_ps[t][:, cols(h)], cand_words, cand_scales, t, z2_codes[:, cols(h)], z2_scales[:, cols(h)], fp4=False)
-            for t in TILES:
-                nc.scalar.copy(b[t][:], b_ps[t][:])
+                    product(b_ps[t // 2][:, t % 2, :], cand_words, cand_scales, t, z2_codes[:, cols(h)], z2_scales[:, cols(h)], fp4=False)
+                for t in TILES:
+                    nc.scalar.copy(b[t][:, cols(h)], b_ps[t // 2][:, t % 2, :])
 
         def differences():
             for h in HALVES:
+                z = work.tile([P, PACK, HALF], BF16, name="z%d" % h, tag=("z0", "z1")[h], align_bytes=64)
                 for t in TILES:
                     fetch("n2", st_near[t][:, cols(h)], st[t], n2_l, h, PACK * h + t)
-                    nc.vector.tensor_tensor(z[:, t, cols(h)], st[t][:, cols(h)], st_near[t][:, cols(h)], ALU.subtract)
+                    nc.gpsimd.tensor_tensor(z[:, t, :], st[t][:, cols(h)], st_near[t][:, cols(h)], ALU.subtract)
                 quantise_half(z, z_grouped, z_codes, z_scales, h)
 
         def layer():
@@ -271,31 +277,36 @@ def tile_picked_tfcdtriebhopgkern_none_po_kernel(
             for t in TILES:
                 nc.scalar.activation(a[t][:], a_ps[t][:], ACT.Copy, scale=0.5)
 
-        def gates():
-            b_sum_ps = banks(0, "b_sum_ps")
+        def score_neighbours(h):
             for t in TILES:
-                for h in HALVES:
-                    fetch("n6", b_near[t][:, cols(h)], b[t], n6_l, h, 2 * t + h)
-                for jb in BLOCKS:
-                    turn_sum(b_sum_ps[t][:, blk(jb)], b[t][:, blk(jb)], b_near[t][:, blk(jb)])
-                nc.scalar.activation(gate_turned[t][:], b_sum_ps[t][:], ACT.Tanh, scale=0.0625 * 0.5)
-            gate = banks(0, "gate")
+                fetch("n6", b_near[t][:, cols(h)], b[t], n6_l, h, PACK * h + t)
+
+        def gate_block(jb):
+            b_sum_ps = psum.tile([P, S], F32, name="b_sum_ps%d" % jb, tag="bank%d" % jb)
             for t in TILES:
-                for jb in BLOCKS:
-                    nc.tensor.transpose(gate[t][:, blk(jb)], gate_turned[t][:, blk(jb)], ident[:])
+                turn_sum(b_sum_ps[:, blk(t)], b[t][:, blk(jb)], b_near[t][:, blk(jb)])
+            nc.scalar.activation(gate_turned[jb][:], b_sum_ps[:], ACT.Tanh, scale=0.0625 * 0.5)
+            gate = psum.tile([P, PACK, P], F32, name="gate%d" % jb, tag="bank%d" % jb)
+            for t in TILES:
+                nc.tensor.transpose(gate[:, t, :], gate_turned[jb][:, blk(t)], ident[:])
             return gate
 
         def pair_sums(h):
             for t in TILES:
-                fetch("n5", a_near[t][:, cols(h)], a[t], n5_l, h, PACK * h + t)
-                nc.vector.tensor_tensor(a_near[t][:, cols(h)], a_near[t][:, cols(h)], a[t][:, cols(h)], ALU.add)
+                fetch("n5", a_near[:, t, cols(h)], a[t], n5_l, h, PACK * h + t)
+                nc.gpsimd.tensor_tensor(a_near[:, t, cols(h)], a_near[:, t, cols(h)], a[t][:, cols(h)], ALU.add)
 
-        def result(h, gate):
-            for t in TILES:
-                nc.vector.scalar_tensor_tensor(res[:, t, cols(h)], gate[t][:, cols(h)], 1.0, a_near[t][:, cols(h)], ALU.add, ALU.mult)
-            nc.sync.dma_start(out_rows[:, :, cols(h)], res[:, :, cols(h)])
-            quantise_half(res, res_grouped, res_codes, res_scales, h, nc.vector.tensor_copy if h else nc.scalar.copy)
-            nc.sync.dma_start(out_words[:, cols(h)], res_codes[:, cols(h)].bitcast(I32))
+        def result(jb, gate):
+            nc.vector.scalar_tensor_tensor(res[:, :, blk(jb)], gate[:], 1.0, a_near[:, :, blk(jb)], ALU.add, ALU.mult)
+            nc.sync.dma_start(out_rows[:, :, blk(jb)], res[:, :, blk(jb)])
+            move = nc.scalar.copy if jb < 0 else nc.vector.tensor_copy
+            move(res_grouped[:, blk(jb), :], res[:, :, blk(jb)].rearrange("p t j -> p j t"))
+            nc.vector.quantize_mx(
+                out=res_codes[:, blk(jb)].bitcast(FP8X4), scales=res_scales[:, blk(jb)],
+                in_=res_grouped[:, blk(jb), :].rearrange("p j t -> p (j t)"),
+            )
+            if jb % 2:
+                nc.sync.dma_start(out_words[:, cols(jb // 2)], res_codes[:, cols(jb // 2)].bitcast(I32))
 
         def store_scales():
             for q in range(4):
@@ -303,25 +314,26 @@ def tile_picked_tfcdtriebhopgkern_none_po_kernel(
 
         for t in TILES:
             nc.scalar.copy(d[t][:], d_ps[t][:])
-        den_ps = banks(0, "den_ps")
-        neighbours(0)
         for t in TILES:
-            if t + 1 < PACK:
-                neighbours(t + 1)
+            neighbours(t)
+        den_ps = banks(0, "den_ps")
+        for t in TILES:
             kernel_weights(t, den_ps)
         for t in TILES:
             nc.scalar.activation(th[t][:], y_ps[t][:], ACT.Tanh, scale=0.5)
-        cand_scales = pick_dealt(xs, cand_l, U8, "cand_scales")
-        cand_words = pick_dealt(xw, cand_l, U32, "cand_words")
-        w3_s = deal_scales(w3_raw_s, "w3_s")
+        cand_scales = pick_dealt(xs, cand_l, U8, "cand_scales", "gap0")
+        cand_words = pick_dealt(xw, cand_l, U32, "cand_words", "gap1")
+        w3_s = deal_scales(w3_raw_s, "w3_s", nc.gpsimd)
         inverse(den_ps)
         for t in TILES:
             gated(t)
         scores(0)
         differences()
         layer()
-        gate = gates()
         for h in HALVES:
             pair_sums(h)
-            result(h, gate)
+        for h in HALVES:
+            score_neighbours(h)
+            for jb in (2 * h, 2 * h + 1):
+                result(jb, gate_block(jb))
         store_scales()

@@ -23,7 +23,7 @@ HALF = S // 2
 HALVES = range(2)
 TILES = range(PACK)
 BLOCKS = range(S // P)
-ON_SCALAR = {"n3": 6, "n4": 0, "n2": 2, "n6": 4, "n5": 2, "n1": 0}
+ON_SCALAR = {"n3": (2,3,4,5,6,7), "n4": (), "n2": (2,3,6,7), "n6": (1,5), "n5": (1,3,5,7), "n1": ()}
 
 
 def tile_picked_tfcdtriebhopgkern_none_po_kernel(
@@ -44,19 +44,19 @@ def tile_picked_tfcdtriebhopgkern_none_po_kernel(
             nc.sync.dma_start(tile[:], src)
             return tile
 
-        def load_scale_rows(tile, src):
+        def load_scale_rows(tile, src, queue=nc.sync):
             nc.vector.memset(tile[:].bitcast(I32), 0)
             for q in range(4):
-                nc.sync.dma_start(tile[32 * q : 32 * q + 4, :].bitcast(I32), src[0, 4 * q : 4 * q + 4, :].bitcast(I32))
+                queue.dma_start(tile[32 * q : 32 * q + 4, :].bitcast(I32), src[0, 4 * q : 4 * q + 4, :].bitcast(I32))
 
         def load_words(words, name):
             raw = held.tile([P, 2 * S], U8, name=name)
             nc.sync.dma_start(raw[:].bitcast(I32), words[0].bitcast(I32))
             return raw
 
-        def load_scales(scales, name):
+        def load_scales(scales, name, queue=nc.sync):
             raw = held.tile([P, S], U8, name=name, align_bytes=64)
-            load_scale_rows(raw, scales)
+            load_scale_rows(raw, scales, queue)
             return raw
 
         def deal_words(raw, name):
@@ -95,7 +95,7 @@ def tile_picked_tfcdtriebhopgkern_none_po_kernel(
 
         def fetch(name, out, window, lst, h, turn, scale=None, bias=None):
             piece = window[:].indirect(half_list(lst, h))
-            on_scalar = (turn + 1) * ON_SCALAR[name] // 8 > turn * ON_SCALAR[name] // 8
+            on_scalar = turn in ON_SCALAR[name]
             if scale is None and on_scalar:
                 nc.scalar.activation(out, piece, ACT.Copy)
             elif scale is None:
@@ -112,8 +112,6 @@ def tile_picked_tfcdtriebhopgkern_none_po_kernel(
             nc.tensor.matmul(out, first, ident[:], start=True, stop=False, is_transpose=True)
             nc.tensor.matmul(out, second, ident[:], start=False, stop=True, is_transpose=True)
 
-        ident = held.tile([P, P], F32, name="ident")
-        make_identity(nc, ident[:])
 
         two_l = load_list(two, "two_l")
         offs_l = load_list(offs, "offs_l")
@@ -124,18 +122,20 @@ def tile_picked_tfcdtriebhopgkern_none_po_kernel(
         w2_raw = load_words(w2_words, "w2_raw")
         w2_raw_s = load_scales(w2_scales, "w2_raw_s")
         w1_raw = load_words(w1_words, "w1_raw")
-        w3_raw = load_words(w3_words, "w3_raw")
+        w1_raw_s = load_scales(w1_scales, "w1_raw_s")
         n3_l = load_list(n3, "n3_l")
         n4_l = load_list(n4, "n4_l")
-        w1_raw_s = load_scales(w1_scales, "w1_raw_s")
-        cand_l = load_list(cand, "cand_l")
+        w3_raw = load_words(w3_words, "w3_raw")
         gs_t = load_row_factor(gs, "gs_t")
+        cand_l = load_list(cand, "cand_l")
         n1_l = load_list(n1, "n1_l")
         gn_t = load_row_factor(gn, "gn_t")
         n2_l = load_list(n2, "n2_l")
         w3_raw_s = load_scales(w3_scales, "w3_raw_s")
         n6_l = load_list(n6, "n6_l")
         n5_l = load_list(n5, "n5_l")
+        ident = held.tile([P, P], F32, name="ident")
+        make_identity(nc, ident[:])
         w2_w = deal_words(w2_raw, "w2_w")
         w1_w = deal_words(w1_raw, "w1_w")
         w3_w = deal_words(w3_raw, "w3_w")
@@ -146,7 +146,7 @@ def tile_picked_tfcdtriebhopgkern_none_po_kernel(
             return picked
 
         def pick_dealt(table, lst, dtype, name, tag):
-            picked = work.tile([P, S], dtype, name=name, tag=tag, align_bytes=64)
+            picked = work.tile([P, S], dtype, name=name, tag=tag, bufs=2, align_bytes=64)
             nc.vector.tensor_copy(picked[:].rearrange("p (t m) -> p m t", t=PACK), table[:].indirect(lst[:]))
             return picked
 
@@ -174,11 +174,12 @@ def tile_picked_tfcdtriebhopgkern_none_po_kernel(
         near = planes("near", width=2 * S)
         gap = planes("gap", width=2 * S)
         kern = planes("kern", width=2 * S)
+        weighed = planes("weighed", width=2 * S)
         th = planes("th")
         sig = planes("sig")
         st = planes("st")
-        st_near = planes("st_near")
         inv = planes("inv")
+        st_near = [work.tile([P, S], F32, name="st_near%d" % t, tag=("inv%d" if t >= 2 else "st_near%d") % t, align_bytes=64) for t in TILES]
         z2_turned = planes("z2_turned", dtype=BF16)
         b = planes("b")
         b_near = planes("b_near")
@@ -213,14 +214,14 @@ def tile_picked_tfcdtriebhopgkern_none_po_kernel(
                 gap[t][:].rearrange("p (u j) -> p u j", u=2), near[t][:].rearrange("p (u j) -> p u j", u=2),
                 d_ps[t][:].unsqueeze(1).to_broadcast([P, 2, S]), ALU.subtract,
             )
-            nc.gpsimd.tensor_scalar(near[t][:], near[t][:], gs_t[:, t : t + 1], 0.0, ALU.mult, ALU.add)
+            nc.gpsimd.tensor_scalar(weighed[t][:], near[t][:], gs_t[:, t : t + 1], 0.0, ALU.mult, ALU.add)
 
         def kernel_weights(t, den_ps):
             nc.scalar.activation(gap[t][:], gap[t][:], ACT.Square)
             nc.scalar.activation(kern[t][:], gap[t][:], ACT.Exp, scale=-0.5)
             for jb in BLOCKS:
                 turn_sum(den_ps[jb][:, blk(t)], kern[t][:, blk(jb)], kern[t][:, blk(PACK + jb)])
-            nc.gpsimd.tensor_tensor(near[t][:], near[t][:], kern[t][:], ALU.mult)
+            nc.gpsimd.tensor_tensor(weighed[t][:], weighed[t][:], kern[t][:], ALU.mult)
 
         def gated(t):
             for h in HALVES:
@@ -237,7 +238,7 @@ def tile_picked_tfcdtriebhopgkern_none_po_kernel(
             num_ps = banks(0, "num_ps")
             for jb in BLOCKS:
                 for t in TILES:
-                    turn_sum(num_ps[jb][:, blk(t)], near[t][:, blk(jb)], near[t][:, blk(PACK + jb)])
+                    turn_sum(num_ps[jb][:, blk(t)], weighed[t][:, blk(jb)], weighed[t][:, blk(PACK + jb)])
             for h in HALVES:
                 for jb in (2 * h, 2 * h + 1):
                     nc.vector.tensor_tensor(
@@ -262,11 +263,12 @@ def tile_picked_tfcdtriebhopgkern_none_po_kernel(
                     nc.scalar.copy(b[t][:, cols(h)], b_ps[t // 2][:, t % 2, :])
 
         def differences():
+            z_halves = work.tile([P, 2, PACK, HALF], BF16, name="z", tag="kern3", align_bytes=64)
             for h in HALVES:
-                z = work.tile([P, PACK, HALF], BF16, name="z%d" % h, tag=("z0", "z1")[h], align_bytes=64)
+                z = z_halves[:, h]
                 for t in TILES:
                     fetch("n2", st_near[t][:, cols(h)], st[t], n2_l, h, PACK * h + t)
-                    nc.gpsimd.tensor_tensor(z[:, t, :], st[t][:, cols(h)], st_near[t][:, cols(h)], ALU.subtract)
+                    (nc.gpsimd if t < 2 else nc.vector).tensor_tensor(z[:, t, :], st[t][:, cols(h)], st_near[t][:, cols(h)], ALU.subtract)
                 quantise_half(z, z_grouped, z_codes, z_scales, h)
 
         def layer():
@@ -294,12 +296,12 @@ def tile_picked_tfcdtriebhopgkern_none_po_kernel(
         def pair_sums(h):
             for t in TILES:
                 fetch("n5", a_near[:, t, cols(h)], a[t], n5_l, h, PACK * h + t)
-                nc.gpsimd.tensor_tensor(a_near[:, t, cols(h)], a_near[:, t, cols(h)], a[t][:, cols(h)], ALU.add)
+                nc.vector.tensor_tensor(a_near[:, t, cols(h)], a_near[:, t, cols(h)], a[t][:, cols(h)], ALU.add)
 
         def result(jb, gate):
             nc.vector.scalar_tensor_tensor(res[:, :, blk(jb)], gate[:], 1.0, a_near[:, :, blk(jb)], ALU.add, ALU.mult)
             nc.sync.dma_start(out_rows[:, :, blk(jb)], res[:, :, blk(jb)])
-            move = nc.scalar.copy if jb < 0 else nc.vector.tensor_copy
+            move = nc.scalar.copy if jb < 3 else nc.vector.tensor_copy
             move(res_grouped[:, blk(jb), :], res[:, :, blk(jb)].rearrange("p t j -> p j t"))
             nc.vector.quantize_mx(
                 out=res_codes[:, blk(jb)].bitcast(FP8X4), scales=res_scales[:, blk(jb)],
@@ -321,9 +323,9 @@ def tile_picked_tfcdtriebhopgkern_none_po_kernel(
             kernel_weights(t, den_ps)
         for t in TILES:
             nc.scalar.activation(th[t][:], y_ps[t][:], ACT.Tanh, scale=0.5)
-        cand_scales = pick_dealt(xs, cand_l, U8, "cand_scales", "gap0")
-        cand_words = pick_dealt(xw, cand_l, U32, "cand_words", "gap1")
-        w3_s = deal_scales(w3_raw_s, "w3_s", nc.gpsimd)
+        cand_scales = pick_dealt(xs, cand_l, U8, "cand_scales", "cs")
+        cand_words = pick_dealt(xw, cand_l, U32, "cand_words", "cw")
+        w3_s = deal_scales(w3_raw_s, "w3_s")
         inverse(den_ps)
         for t in TILES:
             gated(t)

from contextlib import ExitStack

import concourse.mybir as mybir
from concourse.masks import make_identity

K, T, S = 512, 2048, 512
FLOPS = 4 * 2 * K * S * S

F32 = mybir.dt.float32
BF16 = mybir.dt.bfloat16
I32 = mybir.dt.int32
U32 = mybir.dt.uint32
U16 = mybir.dt.uint16
U8 = mybir.dt.uint8
FP8X4 = mybir.dt.float8_e4m3fn_x4
FP4X4 = mybir.dt.float4_e2m1fn_x4
ALU = mybir.AluOpType
ACT = mybir.ActivationFunctionType

P = 128
PACK = 4
HALF = S // 2
HALVES = range(2)
TILES = range(PACK)
BLOCKS = range(S // P)
ON_SCALAR = {"n3": (2,3,4,5,6,7), "n4": (), "n2": (2,3,6,7), "n6": (1,5), "n5": (1,3,5,7), "n1": ()}


def tile_picked_tfcdtriebhopgkern_none_po_kernel(
    tc, x_words, x_scales, w1_words, w1_scales, w2_words, w2_scales, gn, w3_words, w3_scales, gs,
    offs, two, n1, n2, n3, n4, cand, n5, n6, out_0, out_1, out_2,
):
    nc = tc.nc
    with ExitStack() as ctx:
        held = ctx.enter_context(tc.tile_pool(name="held", bufs=1))
        work = ctx.enter_context(tc.tile_pool(name="work", bufs=1))
        psum = ctx.enter_context(tc.psum_pool(name="psum", bufs=1))

        def cols(h):
            return slice(h * HALF, (h + 1) * HALF)

        def load_list(src, name):
            tile = held.tile([P, S // 16], U16, name=name)
            nc.sync.dma_start(tile[:], src)
            return tile

        def load_scale_rows(tile, src, queue=nc.sync):
            nc.vector.memset(tile[:].bitcast(I32), 0)
            for q in range(4):
                queue.dma_start(tile[32 * q : 32 * q + 4, :].bitcast(I32), src[0, 4 * q : 4 * q + 4, :].bitcast(I32))

        def load_words(words, name):
            raw = held.tile([P, 2 * S], U8, name=name)
            nc.sync.dma_start(raw[:].bitcast(I32), words[0].bitcast(I32))
            return raw

        def load_scales(scales, name, queue=nc.sync):
            raw = held.tile([P, S], U8, name=name, align_bytes=64)
            load_scale_rows(raw, scales, queue)
            return raw

        def deal_words(raw, name):
            words = held.tile([P, 2 * S], U8, name=name, align_bytes=64)
            nc.scalar.copy(
                words[:].bitcast(U16).rearrange("p (t m) -> p t m", t=PACK), raw[:].bitcast(U16).rearrange("p (m t) -> p t m", t=PACK),
            )
            return words

        def deal_scales(raw, name, engine=nc.vector):
            scales = held.tile([P, S], U8, name=name, align_bytes=64)
            engine.tensor_copy(scales[:].rearrange("p (t m) -> p t m", t=PACK), raw[:].rearrange("p (m t) -> p t m", t=PACK))
            return scales

        def load_row_factor(src, name):
            tile = held.tile([P, PACK], F32, name=name)
            nc.sync.dma_start(tile[:], src.rearrange("(p t) one -> p (t one)", t=PACK))
            return tile

        def half_list(lst, h):
            return lst[:, h * HALF // 16 : (h + 1) * HALF // 16]

        def planes(name, dtype=F32, width=S, tag=None):
            return [work.tile([P, width], dtype, name="%s%d" % (name, t), tag="%s%d" % (tag or name, t), align_bytes=64) for t in TILES]

        def banks(first, name):
            return [psum.tile([P, S], F32, name="%s%d" % (name, t), tag="bank%d" % (first + t)) for t in TILES]

        def quantise_half(rows, grouped, codes, scales, h, move=nc.vector.tensor_copy):
            move(grouped[:, cols(h), :], rows[:].rearrange("p t j -> p j t"))
            nc.vector.quantize_mx(
                out=codes[:, cols(h)].bitcast(FP8X4),
                scales=scales[:, cols(h)],
                in_=grouped[:, cols(h), :].rearrange("p j t -> p (j t)"),
            )

        def fetch(name, out, window, lst, h, turn, scale=None, bias=None):
            piece = window[:].indirect(half_list(lst, h))
            on_scalar = turn in ON_SCALAR[name]
            if scale is None and on_scalar:
                nc.scalar.activation(out, piece, ACT.Copy)
            elif scale is None:
                nc.vector.tensor_copy(out, piece)
            elif on_scalar:
                nc.scalar.activation(out, piece, ACT.Copy, scale=scale, bias=bias)
            else:
                nc.vector.tensor_scalar(out, piece, scale, bias, ALU.mult, ALU.add)

        def blk(jb):
            return slice(jb * P, (jb + 1) * P)

        def turn_sum(out, first, second):
            nc.tensor.matmul(out, first, ident[:], start=True, stop=False, is_transpose=True)
            nc.tensor.matmul(out, second, ident[:], start=False, stop=True, is_transpose=True)


        two_l = load_list(two, "two_l")
        offs_l = load_list(offs, "offs_l")
        xs = held.tile([P, T], U8, name="xs")
        load_scale_rows(xs, x_scales)
        xw = held.tile([P, T], U32, name="xw")
        nc.sync.dma_start(xw[:].bitcast(I32), x_words[0].rearrange("p n t -> p (n t)").bitcast(I32))
        w2_raw = load_words(w2_words, "w2_raw")
        w2_raw_s = load_scales(w2_scales, "w2_raw_s")
        w1_raw = load_words(w1_words, "w1_raw")
        w1_raw_s = load_scales(w1_scales, "w1_raw_s")
        n3_l = load_list(n3, "n3_l")
        n4_l = load_list(n4, "n4_l")
        w3_raw = load_words(w3_words, "w3_raw")
        gs_t = load_row_factor(gs, "gs_t")
        cand_l = load_list(cand, "cand_l")
        n1_l = load_list(n1, "n1_l")
        gn_t = load_row_factor(gn, "gn_t")
        n2_l = load_list(n2, "n2_l")
        w3_raw_s = load_scales(w3_scales, "w3_raw_s")
        n6_l = load_list(n6, "n6_l")
        n5_l = load_list(n5, "n5_l")
        ident = held.tile([P, P], F32, name="ident")
        make_identity(nc, ident[:])
        w2_w = deal_words(w2_raw, "w2_w")
        w1_w = deal_words(w1_raw, "w1_w")
        w3_w = deal_words(w3_raw, "w3_w")

        def pick(table, lst, dtype, name, tag=None):
            picked = held.tile([P, S], dtype, name=name, tag=tag or name, align_bytes=64)
            nc.vector.tensor_copy(picked[:], table[:].indirect(lst[:]))
            return picked

        def pick_dealt(table, lst, dtype, name, tag):
            picked = work.tile([P, S], dtype, name=name, tag=tag, bufs=2, align_bytes=64)
            nc.vector.tensor_copy(picked[:].rearrange("p (t m) -> p m t", t=PACK), table[:].indirect(lst[:]))
            return picked

        def product(out, words, scales, t, codes, code_scales, fp4=True):
            width = 2 * P if fp4 else P
            nc.tensor.matmul_mx(
                out=out, lhsT=words[:, width * t : width * (t + 1)].bitcast(FP4X4 if fp4 else FP8X4), lhsT_scale=scales[:, blk(t)],
                rhs=codes.bitcast(FP8X4), rhs_scale=code_scales, start=True, stop=True,
            )

        two_scales = pick(xs, two_l, U8, "two_scales")
        two_words = pick(xw, two_l, U32, "two_words")
        w2_s = deal_scales(w2_raw_s, "w2_s")
        d_ps = banks(0, "d_ps")
        for t in TILES:
            product(d_ps[t][:], w2_w, w2_s, t, two_words[:], two_scales[:])
        idx_scales = pick(xs, offs_l, U8, "idx_scales")
        idx_words = pick(xw, offs_l, U32, "idx_words", tag="w2_raw_s")
        w1_s = deal_scales(w1_raw_s, "w1_s")
        y_ps = banks(4, "y_ps")
        for t in TILES:
            product(y_ps[t][:], w1_w, w1_s, t, idx_words[:], idx_scales[:])

        d = planes("d")
        near = planes("near", width=2 * S)
        gap = planes("gap", width=2 * S)
        kern = planes("kern", width=2 * S)
        weighed = planes("weighed", width=2 * S)
        th = planes("th")
        sig = planes("sig")
        st = planes("st")
        inv = planes("inv")
        st_near = [work.tile([P, S], F32, name="st_near%d" % t, tag=("inv%d" if t >= 2 else "st_near%d") % t, align_bytes=64) for t in TILES]
        z2_turned = planes("z2_turned", dtype=BF16)
        b = planes("b")
        b_near = planes("b_near")
        gate_turned = planes("gate_turned")
        a = planes("a")
        a_near = work.tile([P, PACK, S], F32, name="a_near")
        res = work.tile([P, PACK, S], F32, name="res")

        def quantised(name):
            grouped = work.tile([P, S, PACK], BF16, name=name + "_grouped", align_bytes=64)
            codes = work.tile([P, S], U32, name=name + "_codes", align_bytes=64)
            scales = work.tile([P, S], U8, name=name + "_scales", align_bytes=64)
            return grouped, codes, scales

        z_grouped, z_codes, z_scales = quantised("z")
        z2_grouped, z2_codes, z2_scales = quantised("z2")
        res_grouped, res_codes, res_scales = quantised("res")
        half_bias = held.tile([P, 1], F32, name="half_bias")
        nc.vector.memset(half_bias[:], 0.5)
        out_rows = out_0.rearrange("(p t) j -> p t j", t=PACK)
        out_words = out_1[0].rearrange("p n t -> p (n t)").bitcast(I32)

        def words_order(ap, pattern):
            return ap.rearrange(pattern + " -> j u p e", u=2, e=2)

        def neighbours(t):
            for h in HALVES:
                fetch("n3", near[t][:, cols(h)], d[t], n3_l, h, 2 * t + h)
            for h in HALVES:
                fetch("n4", near[t][:, cols(2 + h)], d[t], n4_l, h, 2 * t + h)
            nc.vector.tensor_tensor(
                gap[t][:].rearrange("p (u j) -> p u j", u=2), near[t][:].rearrange("p (u j) -> p u j", u=2),
                d_ps[t][:].unsqueeze(1).to_broadcast([P, 2, S]), ALU.subtract,
            )
            nc.gpsimd.tensor_scalar(weighed[t][:], near[t][:], gs_t[:, t : t + 1], 0.0, ALU.mult, ALU.add)

        def kernel_weights(t, den_ps):
            nc.scalar.activation(gap[t][:], gap[t][:], ACT.Square)
            nc.scalar.activation(kern[t][:], gap[t][:], ACT.Exp, scale=-0.5)
            for jb in BLOCKS:
                turn_sum(den_ps[jb][:, blk(t)], kern[t][:, blk(jb)], kern[t][:, blk(PACK + jb)])
            nc.gpsimd.tensor_tensor(weighed[t][:], weighed[t][:], kern[t][:], ALU.mult)

        def gated(t):
            for h in HALVES:
                fetch("n1", sig[t][:, cols(h)], th[t], n1_l, h, 2 * t + h, 0.5, 0.5)
            nc.vector.scalar_tensor_tensor(st[t][:], y_ps[t][:], gn_t[:, t : t + 1], sig[t][:], ALU.mult, ALU.mult)

        def inverse(den_ps):
            for jb in BLOCKS:
                nc.scalar.activation(words_order(inv[jb][:], "j (u p e)"), words_order(den_ps[jb][:], "j (u e p)"), ACT.Ln, bias=half_bias[:])
            for jb in BLOCKS:
                nc.scalar.activation(inv[jb][:], inv[jb][:], ACT.Exp, scale=-1.0)

        def scores(first_bank):
            num_ps = banks(0, "num_ps")
            for jb in BLOCKS:
                for t in TILES:
                    turn_sum(num_ps[jb][:, blk(t)], weighed[t][:, blk(jb)], weighed[t][:, blk(PACK + jb)])
            for h in HALVES:
                for jb in (2 * h, 2 * h + 1):
                    nc.vector.tensor_tensor(
                        words_order(z2_turned[jb][:], "j (u p e)"), words_order(num_ps[jb][:], "j (u e p)"),
                        words_order(inv[jb][:], "j (u p e)"), ALU.mult,
                    )
                pairs_ps = psum.tile([P, 2, 2, P], F32, name="pairs_ps%d" % h, tag="bank%d" % (2 * h))
                for c in range(2):
                    for u in range(2):
                        nc.tensor.transpose(pairs_ps[:, c, u, :], z2_turned[2 * h + c][:].bitcast(F32)[:, blk(u)], ident[:])
                nc.scalar.copy(
                    z2_grouped[:, cols(h), :].bitcast(F32).rearrange("p (c j) u -> p c j u", c=2), pairs_ps[:].rearrange("p c u j -> p c j u"),
                )
                nc.vector.quantize_mx(
                    out=z2_codes[:, cols(h)].bitcast(FP8X4), scales=z2_scales[:, cols(h)],
                    in_=z2_grouped[:, cols(h), :].rearrange("p j t -> p (j t)"),
                )
                b_ps = [psum.tile([P, 2, HALF], F32, name="b_ps%d%d" % (h, c), tag="bank%d" % (2 * h + c)) for c in range(2)]
                for t in TILES:
                    product(b_ps[t // 2][:, t % 2, :], cand_words, cand_scales, t, z2_codes[:, cols(h)], z2_scales[:, cols(h)], fp4=False)
                for t in TILES:
                    nc.scalar.copy(b[t][:, cols(h)], b_ps[t // 2][:, t % 2, :])

        def differences():
            z_halves = work.tile([P, 2, PACK, HALF], BF16, name="z", tag="kern3", align_bytes=64)
            for h in HALVES:
                z = z_halves[:, h]
                for t in TILES:
                    fetch("n2", st_near[t][:, cols(h)], st[t], n2_l, h, PACK * h + t)
                    (nc.gpsimd if t < 2 else nc.vector).tensor_tensor(z[:, t, :], st[t][:, cols(h)], st_near[t][:, cols(h)], ALU.subtract)
                quantise_half(z, z_grouped, z_codes, z_scales, h)

        def layer():
            a_ps = banks(4, "a_ps")
            for h in HALVES:
                for t in TILES:
                    product(a_ps[t][:, cols(h)], w3_w, w3_s, t, z_codes[:, cols(h)], z_scales[:, cols(h)])
            for t in TILES:
                nc.scalar.activation(a[t][:], a_ps[t][:], ACT.Copy, scale=0.5)

        def score_neighbours(h):
            for t in TILES:
                fetch("n6", b_near[t][:, cols(h)], b[t], n6_l, h, PACK * h + t)

        def gate_block(jb):
            b_sum_ps = psum.tile([P, S], F32, name="b_sum_ps%d" % jb, tag="bank%d" % jb)
            for t in TILES:
                turn_sum(b_sum_ps[:, blk(t)], b[t][:, blk(jb)], b_near[t][:, blk(jb)])
            nc.scalar.activation(gate_turned[jb][:], b_sum_ps[:], ACT.Tanh, scale=0.0625 * 0.5)
            gate = psum.tile([P, PACK, P], F32, name="gate%d" % jb, tag="bank%d" % jb)
            for t in TILES:
                nc.tensor.transpose(gate[:, t, :], gate_turned[jb][:, blk(t)], ident[:])
            return gate

        def pair_sums(h):
            for t in TILES:
                fetch("n5", a_near[:, t, cols(h)], a[t], n5_l, h, PACK * h + t)
                nc.vector.tensor_tensor(a_near[:, t, cols(h)], a_near[:, t, cols(h)], a[t][:, cols(h)], ALU.add)

        def result(jb, gate):
            nc.vector.scalar_tensor_tensor(res[:, :, blk(jb)], gate[:], 1.0, a_near[:, :, blk(jb)], ALU.add, ALU.mult)
            nc.sync.dma_start(out_rows[:, :, blk(jb)], res[:, :, blk(jb)])
            move = nc.scalar.copy if jb < 3 else nc.vector.tensor_copy
            move(res_grouped[:, blk(jb), :], res[:, :, blk(jb)].rearrange("p t j -> p j t"))
            nc.vector.quantize_mx(
                out=res_codes[:, blk(jb)].bitcast(FP8X4), scales=res_scales[:, blk(jb)],
                in_=res_grouped[:, blk(jb), :].rearrange("p j t -> p (j t)"),
            )
            if jb % 2:
                nc.sync.dma_start(out_words[:, cols(jb // 2)], res_codes[:, cols(jb // 2)].bitcast(I32))

        def store_scales():
            for q in range(4):
                nc.scalar.dma_start(out_2[0, 4 * q : 4 * q + 4, :].bitcast(I32), res_scales[32 * q : 32 * q + 4, :].bitcast(I32))

        for t in TILES:
            nc.scalar.copy(d[t][:], d_ps[t][:])
        for t in TILES:
            neighbours(t)
        den_ps = banks(0, "den_ps")
        for t in TILES:
            kernel_weights(t, den_ps)
        for t in TILES:
            nc.scalar.activation(th[t][:], y_ps[t][:], ACT.Tanh, scale=0.5)
        cand_scales = pick_dealt(xs, cand_l, U8, "cand_scales", "cs")
        cand_words = pick_dealt(xw, cand_l, U32, "cand_words", "cw")
        w3_s = deal_scales(w3_raw_s, "w3_s")
        inverse(den_ps)
        for t in TILES:
            gated(t)
        scores(0)
        differences()
        layer()
        for h in HALVES:
            pair_sums(h)
        for h in HALVES:
            score_neighbours(h)
            for jb in (2 * h, 2 * h + 1):
                result(jb, gate_block(jb))
        store_scales()
